import numpy as np
import ml_dtypes


def mxq(x, axis, fmt="e4m3"):
    dtype, down = {"e4m3": (ml_dtypes.float8_e4m3fn, 7), "e5m2": (ml_dtypes.float8_e5m2, 14)}[fmt]
    v = np.moveaxis(np.asarray(x, np.float32).astype(ml_dtypes.bfloat16).astype(np.float64), axis, -1)
    blocks = v.reshape(v.shape[:-1] + (-1, 32))
    amax = np.abs(blocks).max(-1, keepdims=True)
    byte = np.maximum(np.where(amax > 0, np.frexp(amax)[1] - 1 + 127, 0) - down, 1)
    scale = np.exp2(byte - 127.0)
    codes = (blocks / scale).astype(np.float32).astype(dtype).astype(np.float64)
    return np.moveaxis((codes * scale).reshape(v.shape), -1, axis)


WIDE = False


def mx_kscale(k):
    if not WIDE:
        return np.ones(k)
    levels = np.array([10, -10, 5, -5, 0])
    if k % 512:
        return np.exp2(np.random.permutation(np.resize(levels, k // 32))).repeat(32)
    a = np.empty((k // 512, 16))
    for p in range(k // 512):
        a[p, :8] = np.random.permutation(np.resize(levels, 8))
        for g in range(8):
            far = levels[np.abs(levels - a[p, g]) >= 10]
            a[p, g + 8] = far[np.random.randint(len(far))]
    return np.exp2(a.ravel()).repeat(32)


BF16 = ml_dtypes.bfloat16


def bf(x):
    return np.asarray(x, np.float32).astype(BF16)


def f64(x):
    return np.asarray(x).astype(np.float64)


N = 1024


def draw0():
    s = mx_kscale(N)
    return {"f": bf(np.random.standard_normal((N, N)) * s[:, None] * s),
            "x": bf(np.random.standard_normal((N, N)) / np.sqrt(N) / s[:, None]),
            "y": bf(np.random.standard_normal((N, N)) * s[:, None]),
            "v": bf(0.5 * np.random.standard_normal(N))}


def core(f, x, y, v):
    xq = mxq(f64(x), 0, "e4m3")
    half = mxq(f64(f), 1, "e4m3") @ xq
    half = half + f64(v)[:, None] * f64(y)
    return xq.T @ mxq(half, 0, "e4m3")


def e4m3fn_bytes(y):
    return np.clip(np.asarray(y, np.float64), -448.0, 448.0).astype(np.float32).astype(ml_dtypes.float8_e4m3fn).view(np.uint8)


def e4m3fn_values(b):
    return np.asarray(b, np.uint8).view(ml_dtypes.float8_e4m3fn).astype(np.float64)


def setup_inputs():
    d = draw0()
    x0 = np.asarray(d['x']).astype(np.float64)
    s = (np.max(np.abs(x0), axis=(1,), keepdims=True) / 448.0).astype(np.float32)
    out = {}
    for k, v in d.items():
        if k == 'x':
            out['x_bytes'] = e4m3fn_bytes(x0 / s.astype(np.float64))
            out['x_scale'] = s
        else:
            out[k] = v
    return out


def reference(f, x_bytes, x_scale, y, v):
    return core(f, e4m3fn_values(x_bytes) * x_scale.astype(np.float64), y, v)

@@ -1,0 +1,331 @@
+from contextlib import ExitStack
+
+import concourse.mybir as mybir
+from concourse.masks import make_identity
+
+N = 1024
+FLOPS = 2 * 2 * N * N * N
+
+F32 = mybir.dt.float32
+BF16 = mybir.dt.bfloat16
+U32 = mybir.dt.uint32
+U8 = mybir.dt.uint8
+FP8 = mybir.dt.float8_e4m3fn
+FP8X4 = mybir.dt.float8_e4m3fn_x4
+COPY = mybir.ActivationFunctionType.Copy
+MULT = mybir.AluOpType.mult
+ADD = mybir.AluOpType.add
+
+P = 128
+G = 2
+T = 4
+Q = 256
+H = 512
+
+
+def tile_loewdin_fock_shift_s7_kernel(tc, f, x_bytes, x_scale, y, v, out):
+    nc = tc.nc
+    x_rows = x_bytes.rearrange("(g p t) j -> g p t j", p=P, t=T)
+    f_rows = f.rearrange("(g p t) b -> g p t b", p=P, t=T)
+    y_rows = y.rearrange("(g p t) j -> g p t j", p=P, t=T)
+
+    with ExitStack() as ctx:
+        keep = ctx.enter_context(tc.tile_pool(name="keep", bufs=1))
+        psum = ctx.enter_context(tc.psum_pool(name="psum", bufs=4))
+        ctx.enter_context(tc.manual_schedule())
+
+        def grid(name, rows, cols, shape, dtype):
+            return [
+                [keep.tile(shape, dtype, name="%s_%d_%d" % (name, a, b), align_bytes=64) for b in range(cols)]
+                for a in range(rows)
+            ]
+
+        xs = keep.tile([P, G * T], F32, name="xs")
+        vb = keep.tile([P, G * T], BF16, name="vb")
+        vf = keep.tile([P, G * T], F32, name="vf")
+        ident = keep.tile([P, P], F32, name="ident")
+        warm = keep.tile([P, 2], F32, name="warm")
+        xb = grid("xb", G, 2, [P, T, H], U8)
+        xw = grid("xw", G, 4, [P, T, Q], BF16)
+        xi = grid("xi", G, 4, [P, Q, T], BF16)
+        xc = grid("xc", G, 4, [P, Q], U32)
+        xk = grid("xk", G, 4, [P, Q], U8)
+        fs = grid("fs", G, 2, [P, 2, N], BF16)
+        fi = grid("fi", G, 2, [P, 2, G * P * T], BF16)
+        fc = grid("fc", G, 2, [P, 2 * G * P], U32)
+        fk = grid("fk", G, 2, [P, 2 * G * P], U8)
+        ys = grid("ys", G, 2, [P, T, H], BF16)
+        vy = grid("vy", G, 2, [P, T, H], F32)
+        hi = grid("hi", G, 4, [P, Q, T], BF16)
+        hc = grid("hc", G, 4, [P, Q], U32)
+        hk = grid("hk", G, 4, [P, Q], U8)
+        os_ = grid("os", 4, 4, [P, 2, Q], F32)
+
+        nc.scalar.dma_start(out=xs[:], in_=x_scale.rearrange("(g p t) o -> p g (t o)", p=P, t=T))
+        nc.scalar.dma_start(out=vb[:], in_=v.rearrange("(g p t) -> p g t", p=P, t=T))
+        for g in range(G):
+            nc.sync.dma_start(out=xb[g][0][:], in_=x_rows[g][:, :, 0:H])
+        for g in range(G):
+            for r in range(2):
+                nc.sync.dma_start(out=fs[g][r][:], in_=f_rows[g][:, 2 * r : 2 * r + 2, :])
+        for g in range(G):
+            nc.sync.dma_start(out=xb[g][1][:], in_=x_rows[g][:, :, H:N])
+        for h in range(2):
+            for g in range(G):
+                nc.sync.dma_start(out=ys[g][h][:], in_=y_rows[g][:, :, h * H : (h + 1) * H])
+
+        nc.vector.memset(warm[:], 0.0)
+        nc.scalar.activation(out=warm[:, 1:2], in_=warm[:, 0:1], func=COPY)
+        make_identity(nc, ident[:])
+
+        def widen_s(g, q, t):
+            src = xb[g][q // 2][:, t, (q % 2) * Q : (q % 2 + 1) * Q].bitcast(FP8)
+            nc.scalar.activation(out=xw[g][q][:, t, :], in_=src, func=COPY, scale=xs[:, g * T + t : g * T + t + 1])
+
+        def widen_v(g, q, t):
+            src = xb[g][q // 2][:, t, (q % 2) * Q : (q % 2 + 1) * Q].bitcast(FP8)
+            nc.vector.tensor_scalar(
+                out=xw[g][q][:, t, :], in0=src, scalar1=xs[:, g * T + t : g * T + t + 1], scalar2=None, op0=MULT
+            )
+
+        def lay(g, q):
+            nc.vector.tensor_copy(
+                out=xi[g][q][:].rearrange("p (c i) t -> p c t i", i=4),
+                in_=xw[g][q][:].rearrange("p t (c i) -> p c t i", i=4),
+            )
+
+        def quant_x(g, q):
+            nc.vector.quantize_mx(
+                out=xc[g][q][:].bitcast(FP8X4), scales=xk[g][q][:], in_=xi[g][q][:].rearrange("p j t -> p (j t)")
+            )
+
+        tps = {}
+
+        def turn(g, t):
+            ps = psum.tile([P, G, 2, P], F32, name="work")
+            words = fs[g][t // 2][:, t % 2, :].bitcast(F32)
+            for c in range(G):
+                for u in range(2):
+                    nc.tensor.transpose(ps[:, c, u, :], words[:, 256 * c + u : 256 * (c + 1) : 2], ident[:])
+            tps[(g, t)] = ps
+
+        def turn_out(g, t, eng):
+            dst = fi[g][t // 2][:, t % 2, :].bitcast(F32).rearrange("p (c r u) -> p c r u", c=G, u=2)
+            eng(out=dst, in_=tps[(g, t)][:].rearrange("p c u r -> p c r u"))
+
+        def quant_f(g, r):
+            nc.vector.quantize_mx(
+                out=fc[g][r][:].bitcast(FP8X4), scales=fk[g][r][:], in_=fi[g][r][:].rearrange("p s k -> p (s k)")
+            )
+
+        def shift_s(g, h, t):
+            nc.scalar.activation(out=vy[g][h][:, t, :], in_=ys[g][h][:, t, :], func=COPY, scale=vf[:, g * T + t : g * T + t + 1])
+
+        def shift_v(g, h, t):
+            nc.vector.tensor_scalar(
+                out=vy[g][h][:, t, :], in0=ys[g][h][:, t, :], scalar1=vf[:, g * T + t : g * T + t + 1], scalar2=None, op0=MULT
+            )
+
+        gps = {}
+
+        def first(g, q, n):
+            ps = psum.tile([P, T, P], F32, name="half")
+            cols = slice(n * P, (n + 1) * P)
+            for t in range(T):
+                for c in range(G):
+                    w = slice((t % 2) * 2 * P + c * P, (t % 2) * 2 * P + (c + 1) * P)
+                    nc.tensor.matmul_mx(
+                        out=ps[:, t, :],
+                        lhsT=fc[g][t // 2][:, w].bitcast(FP8X4),
+                        lhsT_scale=fk[g][t // 2][:, w],
+                        rhs=xc[c][q][:, cols].bitcast(FP8X4),
+                        rhs_scale=xk[c][q][:, cols],
+                        start=(c == 0),
+                        stop=(c == G - 1),
+                    )
+            gps[(g, q, n)] = ps
+
+        def shifted(g, q, n):
+            j0 = (q % 2) * Q + n * P
+            nc.vector.tensor_tensor(
+                out=hi[g][q][:, n * P : (n + 1) * P, :].rearrange("p (c i) t -> p c t i", i=4),
+                in0=gps[(g, q, n)][:].rearrange("p t (c i) -> p c t i", i=4),
+                in1=vy[g][q // 2][:, :, j0 : j0 + P].rearrange("p t (c i) -> p c t i", i=4),
+                op=ADD,
+            )
+
+        def quant_h_part(g, n):
+            w = slice(n * P, (n + 1) * P)
+            nc.vector.quantize_mx(
+                out=hc[g][3][:, w].bitcast(FP8X4),
+                scales=hk[g][3][:, w],
+                in_=hi[g][3][:, w, :].rearrange("p j t -> p (j t)"),
+            )
+
+        def second_part(n, r):
+            ps = psum.tile([P, 4, P], F32, name="work")
+            cols = slice(n * P, (n + 1) * P)
+            for i in range(4):
+                w = slice((i % 2) * P, (i % 2 + 1) * P)
+                x_at = 2 * r + i // 2
+                for g in range(G):
+                    nc.tensor.matmul_mx(
+                        out=ps[:, i, :],
+                        lhsT=xc[g][x_at][:, w].bitcast(FP8X4),
+                        lhsT_scale=xk[g][x_at][:, w],
+                        rhs=hc[g][3][:, cols].bitcast(FP8X4),
+                        rhs_scale=hk[g][3][:, cols],
+                        start=(g == 0),
+                        stop=(g == G - 1),
+                    )
+            ops[("part", n, r)] = ps
+
+        def finish_part(n, r, eng):
+            dst = os_[3][2 * n + r]
+            eng(out=dst[:].rearrange("p a b -> p (a b)"), in_=ops[("part", n, r)][:].rearrange("p a b -> p (a b)"))
+            j0 = 3 * Q + n * P
+            nc.sync.dma_start(
+                out=out[4 * r * P : 4 * (r + 1) * P, j0 : j0 + P].rearrange("(i p) j -> p i j", p=P),
+                in_=dst[:].rearrange("p a b -> p (a b)").rearrange("p (i j) -> p i j", i=4),
+            )
+
+        def quant_h(g, q):
+            nc.vector.quantize_mx(
+                out=hc[g][q][:].bitcast(FP8X4), scales=hk[g][q][:], in_=hi[g][q][:].rearrange("p j t -> p (j t)")
+            )
+
+        ops = {}
+
+        def second(q, r):
+            ps = psum.tile([P, 2, Q], F32, name="work")
+            for i in range(2):
+                w = slice(i * P, (i + 1) * P)
+                for g in range(G):
+                    nc.tensor.matmul_mx(
+                        out=ps[:, i, :],
+                        lhsT=xc[g][r][:, w].bitcast(FP8X4),
+                        lhsT_scale=xk[g][r][:, w],
+                        rhs=hc[g][q][:].bitcast(FP8X4),
+                        rhs_scale=hk[g][q][:],
+                        start=(g == 0),
+                        stop=(g == G - 1),
+                    )
+            ops[(q, r)] = ps
+
+        def finish(q, r, eng):
+            eng(out=os_[q][r][:], in_=ops[(q, r)][:])
+            nc.sync.dma_start(
+                out=out[2 * r * P : 2 * (r + 1) * P, q * Q : (q + 1) * Q].rearrange("(i p) j -> p i j", p=P),
+                in_=os_[q][r][:],
+            )
+
+        cv = nc.vector.tensor_copy
+        cs = nc.scalar.copy
+
+        def widen(q, engines):
+            for g in range(G):
+                for t in range(T):
+                    if t in engines:
+                        widen_v(g, q, t)
+                    else:
+                        widen_s(g, q, t)
+
+        VT = (2, 3)
+        widen(0, VT)
+        nc.vector.tensor_copy(out=vf[:], in_=vb[:])
+        lay(0, 0)
+        lay(1, 0)
+        widen(1, VT)
+        quant_x(0, 0)
+        quant_x(1, 0)
+        for t in range(T):
+            turn(0, t)
+        for t in range(4):
+            turn_out(0, t, cs)
+        lay(0, 1)
+        quant_f(0, 0)
+        lay(1, 1)
+        quant_f(0, 1)
+        quant_x(0, 1)
+        quant_x(1, 1)
+        for t in range(T):
+            turn(1, t)
+        for n in range(2):
+            first(0, 0, n)
+        for t in range(4):
+            turn_out(1, t, cs)
+        widen(2, (3,))
+        quant_f(1, 0)
+        lay(0, 2)
+        quant_f(1, 1)
+        for n in range(2):
+            first(1, 0, n)
+        for g in range(G):
+            for t in range(2):
+                shift_s(g, 0, t)
+                shift_v(g, 0, t + 2)
+        for g in range(G):
+            for n in range(2):
+                first(g, 1, n)
+        shifted(0, 0, 0)
+        shifted(0, 0, 1)
+        shifted(1, 0, 0)
+        quant_h(0, 0)
+        shifted(1, 0, 1)
+        lay(1, 2)
+        quant_h(1, 0)
+        quant_x(0, 2)
+        quant_x(1, 2)
+        widen(3, ())
+        for r in range(2):
+            second(0, r)
+            finish(0, r, cs)
+        shifted(0, 1, 0)
+        shifted(0, 1, 1)
+        shifted(1, 1, 0)
+        quant_h(0, 1)
+        shifted(1, 1, 1)
+        lay(0, 3)
+        quant_h(1, 1)
+        lay(1, 3)
+        quant_x(0, 3)
+        quant_x(1, 3)
+        for g in range(G):
+            for n in range(2):
+                first(g, 2, n)
+        for g in range(G):
+            for t in range(4):
+                shift_s(g, 1, t)
+        for r in range(2):
+            second(1, r)
+            finish(1, r, cs)
+        for r in range(2, 4):
+            second(0, r)
+            finish(0, r, cs)
+        for g in range(G):
+            for n in range(2):
+                first(g, 3, n)
+        for r in range(2, 4):
+            second(1, r)
+            finish(1, r, cs)
+        shifted(0, 2, 0)
+        shifted(0, 2, 1)
+        shifted(1, 2, 0)
+        quant_h(0, 2)
+        shifted(1, 2, 1)
+        shifted(0, 3, 0)
+        quant_h(1, 2)
+        shifted(1, 3, 0)
+        quant_h_part(0, 0)
+        shifted(0, 3, 1)
+        quant_h_part(1, 0)
+        shifted(1, 3, 1)
+        quant_h_part(0, 1)
+        quant_h_part(1, 1)
+        for r in range(4):
+            second(2, r)
+            finish(2, r, cs)
+        for n in range(2):
+            for r in range(2):
+                second_part(n, r)
+                finish_part(n, r, cv if r == 0 else cs)

@@ -45,6 +45,7 @@ def tile_loewdin_fock_shift_s7_kernel(tc, f, x_bytes, x_scale, y, v, out):
         vf = keep.tile([P, G * T], F32, name="vf")
         ident = keep.tile([P, P], F32, name="ident")
         warm = keep.tile([P, 2], F32, name="warm")
+        dz = keep.tile([P, H], BF16, name="dz", align_bytes=64)
         xb = grid("xb", G, 2, [P, T, H], U8)
         xw = grid("xw", G, 4, [P, T, Q], BF16)
         xi = grid("xi", G, 4, [P, Q, T], BF16)
@@ -63,20 +64,29 @@ def tile_loewdin_fock_shift_s7_kernel(tc, f, x_bytes, x_scale, y, v, out):
 
         nc.scalar.dma_start(out=xs[:], in_=x_scale.rearrange("(g p t) o -> p g (t o)", p=P, t=T))
         nc.scalar.dma_start(out=vb[:], in_=v.rearrange("(g p t) -> p g t", p=P, t=T))
-        for g in range(G):
-            nc.sync.dma_start(out=xb[g][0][:], in_=x_rows[g][:, :, 0:H])
-        for g in range(G):
-            for r in range(2):
-                nc.sync.dma_start(out=fs[g][r][:], in_=f_rows[g][:, 2 * r : 2 * r + 2, :])
-        for g in range(G):
-            nc.sync.dma_start(out=xb[g][1][:], in_=x_rows[g][:, :, H:N])
-        for h in range(2):
-            for g in range(G):
-                nc.sync.dma_start(out=ys[g][h][:], in_=y_rows[g][:, :, h * H : (h + 1) * H])
+        nc.sync.dma_start(out=xb[0][0][:], in_=x_rows[0][:, :, 0*H:0*H+H])
+        nc.sync.dma_start(out=xb[1][0][:], in_=x_rows[1][:, :, 0*H:0*H+H])
+        nc.sync.dma_start(out=fs[1][1][:], in_=f_rows[1][:, 2:4, :])
+        nc.sync.dma_start(out=fs[0][1][:], in_=f_rows[0][:, 2:4, :])
+        nc.sync.dma_start(out=fs[0][0][:], in_=f_rows[0][:, 0:2, :])
+        nc.sync.dma_start(out=fs[1][0][:], in_=f_rows[1][:, 0:2, :])
+        nc.sync.dma_start(out=ys[0][0][:], in_=y_rows[0][:, :, 0*H:0*H+H])
+        nc.sync.dma_start(out=ys[1][0][:], in_=y_rows[1][:, :, 0*H:0*H+H])
+        nc.sync.dma_start(out=xb[1][1][:], in_=x_rows[1][:, :, 1*H:1*H+H])
+        nc.sync.dma_start(out=xb[0][1][:], in_=x_rows[0][:, :, 1*H:1*H+H])
+        nc.sync.dma_start(out=ys[0][1][:], in_=y_rows[0][:, :, 1*H:1*H+H])
+        nc.sync.dma_start(out=ys[1][1][:], in_=y_rows[1][:, :, 1*H:1*H+H])
 
+        nc.vector.memset(dz[:], 0.0)
         nc.vector.memset(warm[:], 0.0)
         nc.scalar.activation(out=warm[:, 1:2], in_=warm[:, 0:1], func=COPY)
         make_identity(nc, ident[:])
+
+        cv = nc.vector.tensor_copy
+        cs = nc.scalar.copy
+
+        def widen(g, q, t, eng):
+            (widen_v if eng == "V" else widen_s)(g, q, t)
 
         def widen_s(g, q, t):
             src = xb[g][q // 2][:, t, (q % 2) * Q : (q % 2 + 1) * Q].bitcast(FP8)
@@ -88,8 +98,8 @@ def tile_loewdin_fock_shift_s7_kernel(tc, f, x_bytes, x_scale, y, v, out):
                 out=xw[g][q][:, t, :], in0=src, scalar1=xs[:, g * T + t : g * T + t + 1], scalar2=None, op0=MULT
             )
 
-        def lay(g, q):
-            nc.vector.tensor_copy(
+        def lay(g, q, eng):
+            (nc.vector.tensor_copy if eng == "V" else nc.scalar.copy)(
                 out=xi[g][q][:].rearrange("p (c i) t -> p c t i", i=4),
                 in_=xw[g][q][:].rearrange("p t (c i) -> p c t i", i=4),
             )
@@ -102,14 +112,15 @@ def tile_loewdin_fock_shift_s7_kernel(tc, f, x_bytes, x_scale, y, v, out):
         tps = {}
 
         def turn(g, t):
-            ps = psum.tile([P, G, 2, P], F32, name="work")
+            ps = psum.tile([P, G, 2, P], F32, name="work_ps", tag="work")
             words = fs[g][t // 2][:, t % 2, :].bitcast(F32)
             for c in range(G):
                 for u in range(2):
                     nc.tensor.transpose(ps[:, c, u, :], words[:, 256 * c + u : 256 * (c + 1) : 2], ident[:])
             tps[(g, t)] = ps
 
-        def turn_out(g, t, eng):
+        def turn_out(g, t, e):
+            eng = {"V": cv, "S": cs}[e]
             dst = fi[g][t // 2][:, t % 2, :].bitcast(F32).rearrange("p (c r u) -> p c r u", c=G, u=2)
             eng(out=dst, in_=tps[(g, t)][:].rearrange("p c u r -> p c r u"))
 
@@ -118,18 +129,27 @@ def tile_loewdin_fock_shift_s7_kernel(tc, f, x_bytes, x_scale, y, v, out):
                 out=fc[g][r][:].bitcast(FP8X4), scales=fk[g][r][:], in_=fi[g][r][:].rearrange("p s k -> p (s k)")
             )
 
-        def shift_s(g, h, t):
-            nc.scalar.activation(out=vy[g][h][:, t, :], in_=ys[g][h][:, t, :], func=COPY, scale=vf[:, g * T + t : g * T + t + 1])
+        def shift(g, h, t, eng):
+            src = ys[g][h][:, t, :]
+            dst = vy[g][h][:, t, :]
+            col = vf[:, g * T + t : g * T + t + 1]
+            if eng == "S":
+                nc.scalar.activation(out=dst, in_=src, func=COPY, scale=col)
+            elif eng == "V":
+                nc.vector.tensor_scalar(out=dst, in0=src, scalar1=col, scalar2=None, op0=MULT)
+            else:
+                nc.gpsimd.tensor_scalar(out=dst, in0=src, scalar1=col, scalar2=0.0, op0=MULT, op1=ADD)
 
-        def shift_v(g, h, t):
-            nc.vector.tensor_scalar(
-                out=vy[g][h][:, t, :], in0=ys[g][h][:, t, :], scalar1=vf[:, g * T + t : g * T + t + 1], scalar2=None, op0=MULT
-            )
+        spin = psum.tile([P, H], F32, name="spin_ps", tag="half")
+
+        def keep_warm(count):
+            for k in range(count):
+                nc.tensor.matmul(spin[:], lhsT=dz[:, 0:P], rhs=dz[:], start=True, stop=True)
 
         gps = {}
 
         def first(g, q, n):
-            ps = psum.tile([P, T, P], F32, name="half")
+            ps = psum.tile([P, T, P], F32, name="half_ps", tag="half")
             cols = slice(n * P, (n + 1) * P)
             for t in range(T):
                 for c in range(G):
@@ -163,7 +183,7 @@ def tile_loewdin_fock_shift_s7_kernel(tc, f, x_bytes, x_scale, y, v, out):
             )
 
         def second_part(n, r):
-            ps = psum.tile([P, 4, P], F32, name="work")
+            ps = psum.tile([P, 4, P], F32, name="work_ps", tag="work")
             cols = slice(n * P, (n + 1) * P)
             for i in range(4):
                 w = slice((i % 2) * P, (i % 2 + 1) * P)
@@ -180,7 +200,8 @@ def tile_loewdin_fock_shift_s7_kernel(tc, f, x_bytes, x_scale, y, v, out):
                     )
             ops[("part", n, r)] = ps
 
-        def finish_part(n, r, eng):
+        def finish_part(n, r, e):
+            eng = {"V": cv, "S": cs}[e]
             dst = os_[3][2 * n + r]
             eng(out=dst[:].rearrange("p a b -> p (a b)"), in_=ops[("part", n, r)][:].rearrange("p a b -> p (a b)"))
             j0 = 3 * Q + n * P
@@ -197,7 +218,7 @@ def tile_loewdin_fock_shift_s7_kernel(tc, f, x_bytes, x_scale, y, v, out):
         ops = {}
 
         def second(q, r):
-            ps = psum.tile([P, 2, Q], F32, name="work")
+            ps = psum.tile([P, 2, Q], F32, name="work_ps", tag="work")
             for i in range(2):
                 w = slice(i * P, (i + 1) * P)
                 for g in range(G):
@@ -212,120 +233,174 @@ def tile_loewdin_fock_shift_s7_kernel(tc, f, x_bytes, x_scale, y, v, out):
                     )
             ops[(q, r)] = ps
 
-        def finish(q, r, eng):
+        def finish(q, r, e):
+            eng = {"V": cv, "S": cs}[e]
             eng(out=os_[q][r][:], in_=ops[(q, r)][:])
             nc.sync.dma_start(
                 out=out[2 * r * P : 2 * (r + 1) * P, q * Q : (q + 1) * Q].rearrange("(i p) j -> p i j", p=P),
                 in_=os_[q][r][:],
             )
 
-        cv = nc.vector.tensor_copy
-        cs = nc.scalar.copy
 
-        def widen(q, engines):
-            for g in range(G):
-                for t in range(T):
-                    if t in engines:
-                        widen_v(g, q, t)
-                    else:
-                        widen_s(g, q, t)
-
-        VT = (2, 3)
-        widen(0, VT)
-        nc.vector.tensor_copy(out=vf[:], in_=vb[:])
-        lay(0, 0)
-        lay(1, 0)
-        widen(1, VT)
-        quant_x(0, 0)
-        quant_x(1, 0)
-        for t in range(T):
-            turn(0, t)
-        for t in range(4):
-            turn_out(0, t, cs)
-        lay(0, 1)
-        quant_f(0, 0)
-        lay(1, 1)
-        quant_f(0, 1)
+        keep_warm(8)
+        widen(0, 0, 3, "V")
+        widen(0, 1, 0, "S")
+        widen(0, 0, 2, "V")
+        widen(0, 0, 0, "S")
+        widen(0, 0, 1, "V")
+        widen(0, 1, 2, "V")
+        widen(0, 1, 3, "S")
+        widen(0, 1, 1, "V")
+        widen(1, 0, 1, "V")
+        widen(1, 1, 3, "S")
+        lay(0, 1, "V")
+        widen(1, 1, 0, "S")
+        widen(1, 0, 0, "S")
+        lay(0, 0, "V")
+        widen(1, 0, 2, "S")
+        turn(1, 3)
+        widen(1, 1, 1, "S")
+        widen(1, 0, 3, "V")
+        widen(1, 1, 2, "S")
+        turn(1, 2)
         quant_x(0, 1)
-        quant_x(1, 1)
-        for t in range(T):
-            turn(1, t)
-        for n in range(2):
-            first(0, 0, n)
-        for t in range(4):
-            turn_out(1, t, cs)
-        widen(2, (3,))
-        quant_f(1, 0)
-        lay(0, 2)
+        turn_out(1, 3, "S")
+        lay(1, 1, "V")
+        turn(0, 2)
+        turn_out(1, 2, "S")
+        lay(1, 0, "V")
+        turn(0, 3)
+        keep_warm(2)
+        turn_out(0, 2, "S")
+        turn(0, 0)
+        quant_x(0, 0)
+        turn_out(0, 3, "S")
         quant_f(1, 1)
-        for n in range(2):
-            first(1, 0, n)
-        for g in range(G):
-            for t in range(2):
-                shift_s(g, 0, t)
-                shift_v(g, 0, t + 2)
-        for g in range(G):
-            for n in range(2):
-                first(g, 1, n)
-        shifted(0, 0, 0)
+        turn(0, 1)
+        turn_out(0, 0, "S")
+        quant_f(0, 1)
+        turn(1, 1)
+        turn_out(0, 1, "S")
+        quant_x(1, 0)
+        turn(1, 0)
+        keep_warm(2)
+        quant_x(1, 1)
+        turn_out(1, 1, "S")
+        quant_f(0, 0)
+        turn_out(1, 0, "S")
+        nc.vector.tensor_copy(out=vf[:], in_=vb[:])
+        shift(0, 0, 1, "V")
+        first(0, 0, 1)
+        shift(0, 0, 2, "V")
+        shift(0, 0, 3, "S")
+        quant_f(1, 0)
+        first(0, 0, 0)
+        shift(0, 0, 0, "S")
+        shift(1, 0, 3, "V")
+        first(1, 0, 0)
+        shift(1, 0, 2, "S")
+        shift(1, 0, 1, "V")
         shifted(0, 0, 1)
+        widen(1, 3, 0, "S")
+        first(1, 0, 1)
+        shift(1, 0, 0, "S")
+        shifted(0, 0, 0)
+        first(1, 1, 0)
+        widen(0, 3, 3, "S")
+        widen(1, 2, 2, "V")
         shifted(1, 0, 0)
-        quant_h(0, 0)
+        widen(0, 2, 2, "S")
+        first(0, 1, 0)
+        widen(0, 3, 0, "S")
         shifted(1, 0, 1)
-        lay(1, 2)
+        widen(0, 2, 1, "S")
+        first(1, 1, 1)
+        widen(0, 2, 0, "S")
+        quant_h(0, 0)
+        widen(0, 2, 3, "S")
         quant_h(1, 0)
-        quant_x(0, 2)
-        quant_x(1, 2)
-        widen(3, ())
-        for r in range(2):
-            second(0, r)
-            finish(0, r, cs)
+        widen(1, 2, 3, "S")
+        lay(0, 2, "V")
+        second(0, 1)
+        widen(1, 3, 1, "S")
+        widen(1, 2, 0, "S")
         shifted(0, 1, 0)
-        shifted(0, 1, 1)
+        second(0, 0)
+        widen(1, 2, 1, "S")
+        finish(0, 1, "S")
+        first(0, 1, 1)
+        lay(1, 2, "V")
+        finish(0, 0, "S")
+        quant_x(0, 2)
+        widen(0, 3, 2, "S")
+        quant_x(1, 2)
+        widen(1, 3, 3, "S")
         shifted(1, 1, 0)
-        quant_h(0, 1)
+        second(0, 2)
+        widen(1, 3, 2, "S")
+        shift(1, 1, 2, "S")
+        shifted(0, 1, 1)
+        first(1, 2, 1)
+        lay(1, 3, "S")
         shifted(1, 1, 1)
-        lay(0, 3)
+        first(1, 2, 0)
+        quant_h(0, 1)
+        first(0, 2, 1)
         quant_h(1, 1)
-        lay(1, 3)
-        quant_x(0, 3)
+        shift(1, 1, 0, "V")
+        shift(1, 1, 3, "S")
+        second(1, 0)
+        widen(0, 3, 1, "V")
         quant_x(1, 3)
-        for g in range(G):
-            for n in range(2):
-                first(g, 2, n)
-        for g in range(G):
-            for t in range(4):
-                shift_s(g, 1, t)
-        for r in range(2):
-            second(1, r)
-            finish(1, r, cs)
-        for r in range(2, 4):
-            second(0, r)
-            finish(0, r, cs)
-        for g in range(G):
-            for n in range(2):
-                first(g, 3, n)
-        for r in range(2, 4):
-            second(1, r)
-            finish(1, r, cs)
-        shifted(0, 2, 0)
-        shifted(0, 2, 1)
-        shifted(1, 2, 0)
-        quant_h(0, 2)
+        shift(1, 1, 1, "S")
+        second(1, 2)
+        lay(0, 3, "V")
+        finish(0, 2, "S")
+        second(1, 1)
         shifted(1, 2, 1)
-        shifted(0, 3, 0)
+        finish(1, 0, "S")
+        first(0, 2, 0)
+        quant_x(0, 3)
+        shift(0, 1, 3, "S")
+        shift(0, 1, 2, "V")
+        second(0, 3)
+        shift(0, 1, 0, "V")
+        shift(0, 1, 1, "S")
+        shifted(1, 2, 0)
+        second(1, 3)
+        finish(1, 2, "S")
+        shifted(0, 2, 1)
+        first(0, 3, 0)
+        finish(1, 1, "S")
+        shifted(0, 2, 0)
+        first(1, 3, 1)
+        finish(0, 3, "S")
         quant_h(1, 2)
-        shifted(1, 3, 0)
-        quant_h_part(0, 0)
-        shifted(0, 3, 1)
-        quant_h_part(1, 0)
+        first(1, 3, 0)
+        quant_h(0, 2)
+        finish(1, 3, "S")
         shifted(1, 3, 1)
-        quant_h_part(0, 1)
+        second(2, 1)
+        shifted(1, 3, 0)
+        second(2, 3)
+        finish(2, 1, "S")
+        shifted(0, 3, 0)
+        second(2, 0)
+        finish(2, 3, "S")
+        quant_h_part(1, 0)
+        second(2, 2)
+        quant_h_part(0, 0)
         quant_h_part(1, 1)
-        for r in range(4):
-            second(2, r)
-            finish(2, r, cs)
-        for n in range(2):
-            for r in range(2):
-                second_part(n, r)
-                finish_part(n, r, cv if r == 0 else cs)
+        finish(2, 0, "S")
+        first(0, 3, 1)
+        finish(2, 2, "S")
+        second_part(0, 1)
+        shifted(0, 3, 1)
+        second_part(0, 0)
+        finish_part(0, 1, "S")
+        quant_h_part(0, 1)
+        second_part(1, 1)
+        finish_part(0, 0, "S")
+        second_part(1, 0)
+        finish_part(1, 1, "S")
+        finish_part(1, 0, "S")

from contextlib import ExitStack

import concourse.mybir as mybir
from concourse.masks import make_identity

N = 1024
FLOPS = 2 * 2 * N * N * N

F32 = mybir.dt.float32
BF16 = mybir.dt.bfloat16
U32 = mybir.dt.uint32
U8 = mybir.dt.uint8
FP8 = mybir.dt.float8_e4m3fn
FP8X4 = mybir.dt.float8_e4m3fn_x4
COPY = mybir.ActivationFunctionType.Copy
MULT = mybir.AluOpType.mult
ADD = mybir.AluOpType.add

P = 128
G = 2
T = 4
Q = 256
H = 512


def tile_loewdin_fock_shift_s7_kernel(tc, f, x_bytes, x_scale, y, v, out):
    nc = tc.nc
    x_rows = x_bytes.rearrange("(g p t) j -> g p t j", p=P, t=T)
    f_rows = f.rearrange("(g p t) b -> g p t b", p=P, t=T)
    y_rows = y.rearrange("(g p t) j -> g p t j", p=P, t=T)

    with ExitStack() as ctx:
        keep = ctx.enter_context(tc.tile_pool(name="keep", bufs=1))
        psum = ctx.enter_context(tc.psum_pool(name="psum", bufs=4))
        ctx.enter_context(tc.manual_schedule())

        def grid(name, rows, cols, shape, dtype):
            return [
                [keep.tile(shape, dtype, name="%s_%d_%d" % (name, a, b), align_bytes=64) for b in range(cols)]
                for a in range(rows)
            ]

        xs = keep.tile([P, G * T], F32, name="xs")
        vb = keep.tile([P, G * T], BF16, name="vb")
        vf = keep.tile([P, G * T], F32, name="vf")
        ident = keep.tile([P, P], F32, name="ident")
        warm = keep.tile([P, 2], F32, name="warm")
        dz = keep.tile([P, H], BF16, name="dz", align_bytes=64)
        xb = grid("xb", G, 2, [P, T, H], U8)
        xw = grid("xw", G, 4, [P, T, Q], BF16)
        xi = grid("xi", G, 4, [P, Q, T], BF16)
        xc = grid("xc", G, 4, [P, Q], U32)
        xk = grid("xk", G, 4, [P, Q], U8)
        fs = grid("fs", G, 2, [P, 2, N], BF16)
        fi = grid("fi", G, 2, [P, 2, G * P * T], BF16)
        fc = grid("fc", G, 2, [P, 2 * G * P], U32)
        fk = grid("fk", G, 2, [P, 2 * G * P], U8)
        ys = grid("ys", G, 2, [P, T, H], BF16)
        vy = grid("vy", G, 2, [P, T, H], F32)
        hi = grid("hi", G, 4, [P, Q, T], BF16)
        hc = grid("hc", G, 4, [P, Q], U32)
        hk = grid("hk", G, 4, [P, Q], U8)
        os_ = grid("os", 4, 4, [P, 2, Q], F32)

        nc.scalar.dma_start(out=xs[:], in_=x_scale.rearrange("(g p t) o -> p g (t o)", p=P, t=T))
        nc.scalar.dma_start(out=vb[:], in_=v.rearrange("(g p t) -> p g t", p=P, t=T))
        nc.sync.dma_start(out=xb[0][0][:], in_=x_rows[0][:, :, 0*H:0*H+H])
        nc.sync.dma_start(out=xb[1][0][:], in_=x_rows[1][:, :, 0*H:0*H+H])
        nc.sync.dma_start(out=fs[1][1][:], in_=f_rows[1][:, 2:4, :])
        nc.sync.dma_start(out=fs[0][1][:], in_=f_rows[0][:, 2:4, :])
        nc.sync.dma_start(out=fs[0][0][:], in_=f_rows[0][:, 0:2, :])
        nc.sync.dma_start(out=fs[1][0][:], in_=f_rows[1][:, 0:2, :])
        nc.sync.dma_start(out=ys[0][0][:], in_=y_rows[0][:, :, 0*H:0*H+H])
        nc.sync.dma_start(out=ys[1][0][:], in_=y_rows[1][:, :, 0*H:0*H+H])
        nc.sync.dma_start(out=xb[1][1][:], in_=x_rows[1][:, :, 1*H:1*H+H])
        nc.sync.dma_start(out=xb[0][1][:], in_=x_rows[0][:, :, 1*H:1*H+H])
        nc.sync.dma_start(out=ys[0][1][:], in_=y_rows[0][:, :, 1*H:1*H+H])
        nc.sync.dma_start(out=ys[1][1][:], in_=y_rows[1][:, :, 1*H:1*H+H])

        nc.vector.memset(dz[:], 0.0)
        nc.vector.memset(warm[:], 0.0)
        nc.scalar.activation(out=warm[:, 1:2], in_=warm[:, 0:1], func=COPY)
        make_identity(nc, ident[:])

        cv = nc.vector.tensor_copy
        cs = nc.scalar.copy

        def widen(g, q, t, eng):
            (widen_v if eng == "V" else widen_s)(g, q, t)

        def widen_s(g, q, t):
            src = xb[g][q // 2][:, t, (q % 2) * Q : (q % 2 + 1) * Q].bitcast(FP8)
            nc.scalar.activation(out=xw[g][q][:, t, :], in_=src, func=COPY, scale=xs[:, g * T + t : g * T + t + 1])

        def widen_v(g, q, t):
            src = xb[g][q // 2][:, t, (q % 2) * Q : (q % 2 + 1) * Q].bitcast(FP8)
            nc.vector.tensor_scalar(
                out=xw[g][q][:, t, :], in0=src, scalar1=xs[:, g * T + t : g * T + t + 1], scalar2=None, op0=MULT
            )

        def lay(g, q, eng):
            (nc.vector.tensor_copy if eng == "V" else nc.scalar.copy)(
                out=xi[g][q][:].rearrange("p (c i) t -> p c t i", i=4),
                in_=xw[g][q][:].rearrange("p t (c i) -> p c t i", i=4),
            )

        def quant_x(g, q):
            nc.vector.quantize_mx(
                out=xc[g][q][:].bitcast(FP8X4), scales=xk[g][q][:], in_=xi[g][q][:].rearrange("p j t -> p (j t)")
            )

        tps = {}

        def turn(g, t):
            ps = psum.tile([P, G, 2, P], F32, name="work_ps", tag="work")
            words = fs[g][t // 2][:, t % 2, :].bitcast(F32)
            for c in range(G):
                for u in range(2):
                    nc.tensor.transpose(ps[:, c, u, :], words[:, 256 * c + u : 256 * (c + 1) : 2], ident[:])
            tps[(g, t)] = ps

        def turn_out(g, t, e):
            eng = {"V": cv, "S": cs}[e]
            dst = fi[g][t // 2][:, t % 2, :].bitcast(F32).rearrange("p (c r u) -> p c r u", c=G, u=2)
            eng(out=dst, in_=tps[(g, t)][:].rearrange("p c u r -> p c r u"))

        def quant_f(g, r):
            nc.vector.quantize_mx(
                out=fc[g][r][:].bitcast(FP8X4), scales=fk[g][r][:], in_=fi[g][r][:].rearrange("p s k -> p (s k)")
            )

        def shift(g, h, t, eng):
            src = ys[g][h][:, t, :]
            dst = vy[g][h][:, t, :]
            col = vf[:, g * T + t : g * T + t + 1]
            if eng == "S":
                nc.scalar.activation(out=dst, in_=src, func=COPY, scale=col)
            elif eng == "V":
                nc.vector.tensor_scalar(out=dst, in0=src, scalar1=col, scalar2=None, op0=MULT)
            else:
                nc.gpsimd.tensor_scalar(out=dst, in0=src, scalar1=col, scalar2=0.0, op0=MULT, op1=ADD)

        spin = psum.tile([P, H], F32, name="spin_ps", tag="half")

        def keep_warm(count):
            for k in range(count):
                nc.tensor.matmul(spin[:], lhsT=dz[:, 0:P], rhs=dz[:], start=True, stop=True)

        gps = {}

        def first(g, q, n):
            ps = psum.tile([P, T, P], F32, name="half_ps", tag="half")
            cols = slice(n * P, (n + 1) * P)
            for t in range(T):
                for c in range(G):
                    w = slice((t % 2) * 2 * P + c * P, (t % 2) * 2 * P + (c + 1) * P)
                    nc.tensor.matmul_mx(
                        out=ps[:, t, :],
                        lhsT=fc[g][t // 2][:, w].bitcast(FP8X4),
                        lhsT_scale=fk[g][t // 2][:, w],
                        rhs=xc[c][q][:, cols].bitcast(FP8X4),
                        rhs_scale=xk[c][q][:, cols],
                        start=(c == 0),
                        stop=(c == G - 1),
                    )
            gps[(g, q, n)] = ps

        def shifted(g, q, n):
            j0 = (q % 2) * Q + n * P
            nc.vector.tensor_tensor(
                out=hi[g][q][:, n * P : (n + 1) * P, :].rearrange("p (c i) t -> p c t i", i=4),
                in0=gps[(g, q, n)][:].rearrange("p t (c i) -> p c t i", i=4),
                in1=vy[g][q // 2][:, :, j0 : j0 + P].rearrange("p t (c i) -> p c t i", i=4),
                op=ADD,
            )

        def quant_h_part(g, n):
            w = slice(n * P, (n + 1) * P)
            nc.vector.quantize_mx(
                out=hc[g][3][:, w].bitcast(FP8X4),
                scales=hk[g][3][:, w],
                in_=hi[g][3][:, w, :].rearrange("p j t -> p (j t)"),
            )

        def second_part(n, r):
            ps = psum.tile([P, 4, P], F32, name="work_ps", tag="work")
            cols = slice(n * P, (n + 1) * P)
            for i in range(4):
                w = slice((i % 2) * P, (i % 2 + 1) * P)
                x_at = 2 * r + i // 2
                for g in range(G):
                    nc.tensor.matmul_mx(
                        out=ps[:, i, :],
                        lhsT=xc[g][x_at][:, w].bitcast(FP8X4),
                        lhsT_scale=xk[g][x_at][:, w],
                        rhs=hc[g][3][:, cols].bitcast(FP8X4),
                        rhs_scale=hk[g][3][:, cols],
                        start=(g == 0),
                        stop=(g == G - 1),
                    )
            ops[("part", n, r)] = ps

        def finish_part(n, r, e):
            eng = {"V": cv, "S": cs}[e]
            dst = os_[3][2 * n + r]
            eng(out=dst[:].rearrange("p a b -> p (a b)"), in_=ops[("part", n, r)][:].rearrange("p a b -> p (a b)"))
            j0 = 3 * Q + n * P
            nc.sync.dma_start(
                out=out[4 * r * P : 4 * (r + 1) * P, j0 : j0 + P].rearrange("(i p) j -> p i j", p=P),
                in_=dst[:].rearrange("p a b -> p (a b)").rearrange("p (i j) -> p i j", i=4),
            )

        def quant_h(g, q):
            nc.vector.quantize_mx(
                out=hc[g][q][:].bitcast(FP8X4), scales=hk[g][q][:], in_=hi[g][q][:].rearrange("p j t -> p (j t)")
            )

        ops = {}

        def second(q, r):
            ps = psum.tile([P, 2, Q], F32, name="work_ps", tag="work")
            for i in range(2):
                w = slice(i * P, (i + 1) * P)
                for g in range(G):
                    nc.tensor.matmul_mx(
                        out=ps[:, i, :],
                        lhsT=xc[g][r][:, w].bitcast(FP8X4),
                        lhsT_scale=xk[g][r][:, w],
                        rhs=hc[g][q][:].bitcast(FP8X4),
                        rhs_scale=hk[g][q][:],
                        start=(g == 0),
                        stop=(g == G - 1),
                    )
            ops[(q, r)] = ps

        def finish(q, r, e):
            eng = {"V": cv, "S": cs}[e]
            eng(out=os_[q][r][:], in_=ops[(q, r)][:])
            nc.sync.dma_start(
                out=out[2 * r * P : 2 * (r + 1) * P, q * Q : (q + 1) * Q].rearrange("(i p) j -> p i j", p=P),
                in_=os_[q][r][:],
            )


        keep_warm(8)
        widen(0, 0, 3, "V")
        widen(0, 1, 0, "S")
        widen(0, 0, 2, "V")
        widen(0, 0, 0, "S")
        widen(0, 0, 1, "V")
        widen(0, 1, 2, "V")
        widen(0, 1, 3, "S")
        widen(0, 1, 1, "V")
        widen(1, 0, 1, "V")
        widen(1, 1, 3, "S")
        lay(0, 1, "V")
        widen(1, 1, 0, "S")
        widen(1, 0, 0, "S")
        lay(0, 0, "V")
        widen(1, 0, 2, "S")
        turn(1, 3)
        widen(1, 1, 1, "S")
        widen(1, 0, 3, "V")
        widen(1, 1, 2, "S")
        turn(1, 2)
        quant_x(0, 1)
        turn_out(1, 3, "S")
        lay(1, 1, "V")
        turn(0, 2)
        turn_out(1, 2, "S")
        lay(1, 0, "V")
        turn(0, 3)
        keep_warm(2)
        turn_out(0, 2, "S")
        turn(0, 0)
        quant_x(0, 0)
        turn_out(0, 3, "S")
        quant_f(1, 1)
        turn(0, 1)
        turn_out(0, 0, "S")
        quant_f(0, 1)
        turn(1, 1)
        turn_out(0, 1, "S")
        quant_x(1, 0)
        turn(1, 0)
        keep_warm(2)
        quant_x(1, 1)
        turn_out(1, 1, "S")
        quant_f(0, 0)
        turn_out(1, 0, "S")
        nc.vector.tensor_copy(out=vf[:], in_=vb[:])
        shift(0, 0, 1, "V")
        first(0, 0, 1)
        shift(0, 0, 2, "V")
        shift(0, 0, 3, "S")
        quant_f(1, 0)
        first(0, 0, 0)
        shift(0, 0, 0, "S")
        shift(1, 0, 3, "V")
        first(1, 0, 0)
        shift(1, 0, 2, "S")
        shift(1, 0, 1, "V")
        shifted(0, 0, 1)
        widen(1, 3, 0, "S")
        first(1, 0, 1)
        shift(1, 0, 0, "S")
        shifted(0, 0, 0)
        first(1, 1, 0)
        widen(0, 3, 3, "S")
        widen(1, 2, 2, "V")
        shifted(1, 0, 0)
        widen(0, 2, 2, "S")
        first(0, 1, 0)
        widen(0, 3, 0, "S")
        shifted(1, 0, 1)
        widen(0, 2, 1, "S")
        first(1, 1, 1)
        widen(0, 2, 0, "S")
        quant_h(0, 0)
        widen(0, 2, 3, "S")
        quant_h(1, 0)
        widen(1, 2, 3, "S")
        lay(0, 2, "V")
        second(0, 1)
        widen(1, 3, 1, "S")
        widen(1, 2, 0, "S")
        shifted(0, 1, 0)
        second(0, 0)
        widen(1, 2, 1, "S")
        finish(0, 1, "S")
        first(0, 1, 1)
        lay(1, 2, "V")
        finish(0, 0, "S")
        quant_x(0, 2)
        widen(0, 3, 2, "S")
        quant_x(1, 2)
        widen(1, 3, 3, "S")
        shifted(1, 1, 0)
        second(0, 2)
        widen(1, 3, 2, "S")
        shift(1, 1, 2, "S")
        shifted(0, 1, 1)
        first(1, 2, 1)
        lay(1, 3, "S")
        shifted(1, 1, 1)
        first(1, 2, 0)
        quant_h(0, 1)
        first(0, 2, 1)
        quant_h(1, 1)
        shift(1, 1, 0, "V")
        shift(1, 1, 3, "S")
        second(1, 0)
        widen(0, 3, 1, "V")
        quant_x(1, 3)
        shift(1, 1, 1, "S")
        second(1, 2)
        lay(0, 3, "V")
        finish(0, 2, "S")
        second(1, 1)
        shifted(1, 2, 1)
        finish(1, 0, "S")
        first(0, 2, 0)
        quant_x(0, 3)
        shift(0, 1, 3, "S")
        shift(0, 1, 2, "V")
        second(0, 3)
        shift(0, 1, 0, "V")
        shift(0, 1, 1, "S")
        shifted(1, 2, 0)
        second(1, 3)
        finish(1, 2, "S")
        shifted(0, 2, 1)
        first(0, 3, 0)
        finish(1, 1, "S")
        shifted(0, 2, 0)
        first(1, 3, 1)
        finish(0, 3, "S")
        quant_h(1, 2)
        first(1, 3, 0)
        quant_h(0, 2)
        finish(1, 3, "S")
        shifted(1, 3, 1)
        second(2, 1)
        shifted(1, 3, 0)
        second(2, 3)
        finish(2, 1, "S")
        shifted(0, 3, 0)
        second(2, 0)
        finish(2, 3, "S")
        quant_h_part(1, 0)
        second(2, 2)
        quant_h_part(0, 0)
        quant_h_part(1, 1)
        finish(2, 0, "S")
        first(0, 3, 1)
        finish(2, 2, "S")
        second_part(0, 1)
        shifted(0, 3, 1)
        second_part(0, 0)
        finish_part(0, 1, "S")
        quant_h_part(0, 1)
        second_part(1, 1)
        finish_part(0, 0, "S")
        second_part(1, 0)
        finish_part(1, 1, "S")
        finish_part(1, 0, "S")
